import numpy as np
import ml_dtypes


def mxq(x, axis, fmt="e4m3"):
    dtype, down = {"e4m3": (ml_dtypes.float8_e4m3fn, 7), "e5m2": (ml_dtypes.float8_e5m2, 14)}[fmt]
    v = np.moveaxis(np.asarray(x, np.float32).astype(ml_dtypes.bfloat16).astype(np.float64), axis, -1)
    blocks = v.reshape(v.shape[:-1] + (-1, 32))
    amax = np.abs(blocks).max(-1, keepdims=True)
    byte = np.maximum(np.where(amax > 0, np.frexp(amax)[1] - 1 + 127, 0) - down, 1)
    scale = np.exp2(byte - 127.0)
    codes = (blocks / scale).astype(np.float32).astype(dtype).astype(np.float64)
    return np.moveaxis((codes * scale).reshape(v.shape), -1, axis)


WIDE = False


def mx_kscale(k):
    if not WIDE:
        return np.ones(k)
    levels = np.array([10, -10, 5, -5, 0])
    if k % 512:
        return np.exp2(np.random.permutation(np.resize(levels, k // 32))).repeat(32)
    a = np.empty((k // 512, 16))
    for p in range(k // 512):
        a[p, :8] = np.random.permutation(np.resize(levels, 8))
        for g in range(8):
            far = levels[np.abs(levels - a[p, g]) >= 10]
            a[p, g + 8] = far[np.random.randint(len(far))]
    return np.exp2(a.ravel()).repeat(32)


BF16 = ml_dtypes.bfloat16


def bf(x):
    return np.asarray(x, np.float32).astype(BF16)


def f64(x):
    return np.asarray(x).astype(np.float64)


E2M1 = np.array([0.0, 0.5, 1.0, 1.5, 2.0, 3.0, 4.0, 6.0, -0.0, -0.5, -1.0, -1.5, -2.0, -3.0, -4.0, -6.0])


def pack_weight(w, fmt):
    k, n = w.shape
    w = f64(bf(w)).reshape(k // 32, 32, n)
    amax = np.abs(w).max(1)
    if fmt == "e4m3":
        byte = np.frexp(amax)[1] - 1 + 127 - 7
    else:
        mant, ex = np.frexp(amax / 6.0)
        byte = np.where(mant > 0.5, ex, ex - 1) + 127
    byte = np.clip(np.where(amax > 0, byte, 1), 1, 254)
    scaled = (w * np.exp2(127.0 - byte)[:, None, :]).reshape(k, n).astype(np.float32)
    by_word = np.ascontiguousarray(scaled.reshape(k // 512, 128, 4, n).transpose(0, 1, 3, 2))
    if fmt == "e4m3":
        words = by_word.astype(ml_dtypes.float8_e4m3fn).view(np.uint8)
    else:
        c = by_word.astype(ml_dtypes.float4_e2m1fn).view(np.uint8) & 0xF
        words = c[..., 0::2] | (c[..., 1::2] << 4)
    return np.ascontiguousarray(words), np.ascontiguousarray(byte.astype(np.uint8).reshape(k // 512, 16, n))


def unpack_weight(words, scales, fmt):
    g, p, n, _ = words.shape
    if fmt == "e4m3":
        vals = np.ascontiguousarray(words).view(ml_dtypes.float8_e4m3fn).astype(np.float64)
    else:
        nib = np.empty((g, p, n, 4), np.uint8)
        nib[..., 0::2] = words & 0xF
        nib[..., 1::2] = words >> 4
        vals = E2M1[nib]
    vals = vals * np.repeat(np.exp2(scales.astype(np.float64) - 127.0), 8, axis=1)[..., None]
    return vals.transpose(0, 1, 3, 2).reshape(g * 512, n)
def pack4(w):
    words, scales = pack_weight(w, "e2m1")
    return words.reshape(words.shape[0], 128, -1), scales


def unpack4(words, scales):
    return unpack_weight(words.reshape(words.shape[0], 128, -1, 2), scales, "e2m1")


E4M3FN = np.array([(-1.0 if i & 128 else 1.0) * ((1.0 + (i & 7) / 8.0) * 2.0 ** (((i >> 3) & 15) - 7) if i & 120 else (i & 7) * 2.0 ** -9) for i in range(256)])


def e4m3fn_bytes(y):
    return np.clip(np.asarray(y, np.float64), -448.0, 448.0).astype(np.float32).astype(ml_dtypes.float8_e4m3fn).view(np.uint8)


def e4m3fn_values(b):
    return E4M3FN[b]


N, D, V, E = 512, 1024, 2048, 1024


def scaled_softmax(logits):
    vocab = logits.shape[-1]
    e = np.exp(logits - logits.max(-1, keepdims=True))
    return vocab * (e / e.sum(-1, keepdims=True))


def residual(p, q):
    d = np.maximum(p - q, 0.0)
    return d / d.mean(-1, keepdims=True)


def draw0():
    s, t = mx_kscale(D), mx_kscale(V)
    h_t = bf(np.random.standard_normal((N, D)) * s)
    w_t_words, w_t_scales = pack4(np.random.standard_normal((D, V)) / np.sqrt(D) / s[:, None])
    q1 = bf(np.random.uniform(0.0, 2.0, (N, V)))
    q2 = bf(np.random.uniform(0.0, 2.0, (N, V)))
    g = bf(np.random.standard_normal(V) * t)
    emb_words, emb_scales = pack4(np.random.standard_normal((V, E)) / np.sqrt(V) / t[:, None])
    return {
        "h_t": h_t,
        "w_t_words": w_t_words,
        "w_t_scales": w_t_scales,
        "q1": q1,
        "q2": q2,
        "g": g,
        "emb_words": emb_words,
        "emb_scales": emb_scales,
    }


def core(h_t, w_t_words, w_t_scales, q1, q2, g, emb_words, emb_scales):
    lt = mxq(f64(h_t), 1, "e4m3") @ unpack4(w_t_words, w_t_scales)
    p = scaled_softmax(lt)
    r1 = residual(p, f64(q1))
    r2 = residual(r1, f64(q2))
    c = r2 * f64(g)[None, :]
    return mxq(c, 1, "e4m3") @ unpack4(emb_words, emb_scales)


def setup_inputs():
    drawn = draw0()
    full = np.asarray(drawn['h_t']).astype(np.float64)
    scale = (np.abs(full).reshape(4, 128, 8, 128).max(axis=(1, 3)) / 448.0).astype(np.float32)
    given = {}
    for key, value in drawn.items():
        if key == 'h_t':
            given['h_t_bytes'] = e4m3fn_bytes(full / np.repeat(np.repeat(scale.astype(np.float64), 128, axis=0), 128, axis=1))
            given['h_t_scale'] = scale
        else:
            given[key] = value
    return given


def reference(h_t_bytes, h_t_scale, w_t_words, w_t_scales, q1, q2, g, emb_words, emb_scales):
    return core(e4m3fn_values(h_t_bytes) * np.repeat(np.repeat(h_t_scale.astype(np.float64), 128, axis=0), 128, axis=1), w_t_words, w_t_scales, q1, q2, g, emb_words, emb_scales)

@@ -1,0 +1,432 @@
+from contextlib import ExitStack
+
+import concourse.mybir as mybir
+from concourse.masks import make_identity
+
+N, D, V, E = 512, 1024, 2048, 1024
+FLOPS = 2 * N * D * V + 2 * N * V * E
+
+F32 = mybir.dt.float32
+BF16 = mybir.dt.bfloat16
+U8 = mybir.dt.uint8
+U32 = mybir.dt.uint32
+I32 = mybir.dt.int32
+FP8 = mybir.dt.float8_e4m3fn
+A4 = mybir.dt.float8_e4m3fn_x4
+W4 = mybir.dt.float4_e2m1fn_x4
+ALU = mybir.AluOpType
+ACT = mybir.ActivationFunctionType
+AX = mybir.AxisListType
+
+P = 128
+TILES = N // P
+CH = 1
+
+
+def tile_specinferrecursiveresidualverify_d2p_kernel(
+    tc, h_t_bytes, h_t_scale, w_t_words, w_t_scales, q1, q2, g, emb_words, emb_scales, out
+):
+    nc = tc.nc
+    with ExitStack() as ctx:
+        keep = ctx.enter_context(tc.tile_pool(name="keep", bufs=1))
+        psum = ctx.enter_context(tc.psum_pool(name="psum", bufs=2))
+        ctx.enter_context(tc.manual_schedule())
+
+        def bank(use):
+            return psum.tile([P, 512], F32, name=use, tag=use, bufs=4 if use == "lt" else 2)
+
+        hb = [keep.tile([P, D], U8, name="hb%d" % i, align_bytes=64) for i in range(TILES)]
+        hs = keep.tile([P, 32], F32, name="hs")
+        hw = [keep.tile([P, D], BF16, name="hw%d" % i, align_bytes=64) for i in range(TILES)]
+        hg = [keep.tile([P, 1024], BF16, name="hg%d" % i, align_bytes=64) for i in range(TILES)]
+        hc = [keep.tile([P, 256], U32, name="hc%d" % i, align_bytes=64) for i in range(TILES)]
+        hcs = [keep.tile([P, 256], U8, name="hcs%d" % i, align_bytes=64) for i in range(TILES)]
+        ww = [keep.tile([P, 2, 1024], U8, name="ww%d" % b, align_bytes=64) for b in range(4)]
+        ws = keep.tile([P, 2, V], U8, name="ws", align_bytes=64)
+        ew = keep.tile([P, 4, 2 * E], U8, name="ew", align_bytes=64)
+        es = keep.tile([P, 4, E], U8, name="es", align_bytes=64)
+        q1t = [keep.tile([P, V], BF16, name="q1t%d" % i) for i in range(TILES)]
+        q2t = [keep.tile([P, V], BF16, name="q2t%d" % i) for i in range(TILES)]
+        gt = keep.tile([P, V], BF16, name="gt")
+        ident = keep.tile([P, P], F32, name="ident")
+        ebuf = [keep.tile([P, V], F32, name="ebuf%d" % i) for i in range(TILES)]
+        ubuf = [keep.tile([P, V], F32, name="ubuf%d" % i) for i in range(TILES)]
+        cbuf = [keep.tile([P, V], BF16, name="cbuf%d" % i, align_bytes=64) for i in range(TILES)]
+        cg = [keep.tile([P, 2048], BF16, name="cg%d" % i, align_bytes=64) for i in range(TILES)]
+        cc = [keep.tile([P, 512], U32, name="cc%d" % i, align_bytes=64) for i in range(TILES)]
+        ccs = [keep.tile([P, 512], U8, name="ccs%d" % i, align_bytes=64) for i in range(TILES)]
+        ot = [keep.tile([P, E], F32, name="ot%d" % i) for i in range(TILES)]
+        mx = [keep.tile([P, 4], F32, name="mx%d" % i) for i in range(TILES)]
+        nm = [keep.tile([P, 1], F32, name="nm%d" % i) for i in range(TILES)]
+        inv = [keep.tile([P, 1], F32, name="inv%d" % i) for i in range(TILES)]
+        eacc = [keep.tile([P, 4], F32, name="eacc%d" % i) for i in range(TILES)]
+        racc = [keep.tile([P, CH], F32, name="racc%d" % i) for i in range(TILES)]
+        tacc = [keep.tile([P, 1 if i < 3 else 2], F32, name="tacc%d" % i) for i in range(TILES)]
+        nsig = [keep.tile([P, 1], F32, name="nsig%d" % i) for i in range(TILES)]
+        nm1 = [keep.tile([P, 1], F32, name="nm1%d" % i) for i in range(TILES)]
+        m2 = [keep.tile([P, 1], F32, name="m2%d" % i) for i in range(TILES)]
+        junk = keep.tile([P, 4], F32, name="junk")
+        warm = keep.tile([P, 1], F32, name="warm")
+
+        nc.scalar.dma_start(out=hs[:], in_=h_t_scale.rearrange("i j -> (i j)").partition_broadcast(P))
+        nc.vector.memset(warm[:], 0.0)
+        nc.scalar.activation(out=warm[:], in_=warm[:], func=ACT.Exp)
+        nc.vector.memset(ws[:].rearrange("p g n -> p (g n)").bitcast(I32), 0)
+        make_identity(nc, ident[:])
+        nc.gpsimd.memset(es[:].rearrange("p g n -> p (g n)").bitcast(I32), 0)
+
+        def load_scales(dst, src):
+            for quad in range(4):
+                nc.sync.dma_start(
+                    out=dst[32 * quad : 32 * quad + 4, :, :].bitcast(I32),
+                    in_=src[:, 4 * quad : 4 * quad + 4, :].rearrange("g r n -> r g n").bitcast(I32),
+                )
+
+        def load_h(i):
+            nc.sync.dma_start(out=hb[i][:], in_=h_t_bytes[P * i : P * (i + 1), :])
+
+        def load_q(dst, src, i):
+            nc.sync.dma_start(out=dst[i][:], in_=src[P * i : P * (i + 1), :])
+
+        wsrc = w_t_words.rearrange("g p c -> p g c")
+
+        def load_w(b):
+            nc.sync.dma_start(out=ww[b][:], in_=wsrc[:, :, 1024 * b : 1024 * (b + 1)])
+
+        load_h(0)
+        load_h(1)
+        load_scales(ws, w_t_scales)
+        load_w(0)
+        load_w(1)
+        load_h(2)
+        load_w(2)
+        load_w(3)
+        load_h(3)
+        load_q(q1t, q1, 0)
+        load_q(q1t, q1, 1)
+        load_q(q2t, q2, 0)
+        load_q(q1t, q1, 2)
+        load_q(q2t, q2, 1)
+        nc.sync.dma_start(out=gt[:], in_=g.partition_broadcast(P))
+        load_q(q1t, q1, 3)
+        load_q(q2t, q2, 2)
+        load_scales(es, emb_scales)
+        nc.sync.dma_start(out=ew[:], in_=emb_words.rearrange("g p c -> p g c"))
+        load_q(q2t, q2, 3)
+
+        def widen(i, blocks, eng):
+            for j in blocks:
+                cols = slice(P * j, P * (j + 1))
+                col = hs[:, 8 * i + j : 8 * i + j + 1]
+                if eng == "v":
+                    nc.vector.tensor_scalar(
+                        out=hw[i][:, cols], in0=hb[i][:, cols].bitcast(FP8), scalar1=col, scalar2=None, op0=ALU.mult
+                    )
+                else:
+                    nc.scalar.activation(out=hw[i][:, cols], in_=hb[i][:, cols].bitcast(FP8), func=ACT.Copy, scale=col)
+
+        def turn(dst, words, k):
+            for s in range(k):
+                for u in range(2):
+                    nc.tensor.transpose(dst[:, s, u, :], words[:, 256 * s + u : 256 * (s + 1) : 2], ident[:])
+
+        def untwist(dst, k):
+            return dst.bitcast(F32).rearrange("p (s r u) -> p s r u", s=k, u=2)
+
+        def twisted(b, k):
+            return b[:, : 256 * k].rearrange("p (s u r) -> p s u r", s=k, u=2)
+
+        hbank = {}
+
+        def h_turn(i, s, k):
+            b = bank("turn")
+            hbank[i, s] = b
+            turn(twisted(b, k), hw[i][:].bitcast(F32)[:, 256 * s : 256 * (s + k)], k)
+
+        def h_copy(i, s, k, eng):
+            dst = untwist(hg[i][:, 512 * s : 512 * (s + k)], k)
+            src = twisted(hbank[i, s], k).rearrange("p s u r -> p s r u")
+            if eng == "v":
+                nc.vector.tensor_copy(out=dst, in_=src)
+            else:
+                nc.scalar.copy(out=dst, in_=src)
+
+        def h_quant(i, s, k):
+            nc.vector.quantize_mx(
+                out=hc[i][:, P * s : P * (s + k)].bitcast(A4),
+                scales=hcs[i][:, P * s : P * (s + k)],
+                in_=hg[i][:, 512 * s : 512 * (s + k)],
+            )
+
+        ltb = {}
+
+        def lt(i, banks=range(4)):
+            for b in banks:
+                t = bank("acc" if i == 1 and b < 2 else "lt")
+                ltb[i, b] = t
+                for s in range(2):
+                    nc.tensor.matmul_mx(
+                        out=t[:],
+                        lhsT=hc[i][:, P * s : P * (s + 1)].bitcast(A4),
+                        lhsT_scale=hcs[i][:, P * s : P * (s + 1)],
+                        rhs=ww[b][:, s, :].bitcast(W4),
+                        rhs_scale=ws[:, s, 512 * b : 512 * (b + 1)],
+                        start=(s == 0),
+                        stop=(s == 1),
+                    )
+
+        def rowmax(i, banks=range(4)):
+            for b in banks:
+                nc.vector.tensor_reduce(out=mx[i][:, b : b + 1], in_=ltb[i, b][:], axis=AX.X, op=ALU.max)
+
+        def negmax(i):
+            nc.vector.tensor_reduce(out=nm[i][:], in_=mx[i][:], axis=AX.X, op=ALU.max, negate=True)
+
+        def mean(dst, acc, sign):
+            n = acc.shape[1]
+            nc.scalar.activation(
+                out=junk[:, :n], in_=acc[:], func=ACT.Copy, scale=sign / V, accum_out=dst[:]
+            )
+
+        def exps(i):
+            for b in range(4):
+                nc.scalar.activation(
+                    out=ebuf[i][:, 512 * b : 512 * (b + 1)],
+                    in_=ltb[i, b][:],
+                    func=ACT.Exp,
+                    bias=nm[i][:],
+                    scale=1.0,
+                    accum_out=eacc[i][:, b : b + 1],
+                )
+            mean(nsig[i], eacc[i], -1.0)
+
+        def chunks():
+            w = V // CH
+            return [(c, slice(w * c, w * (c + 1))) for c in range(CH)]
+
+        def sub1(i, lo=0, hi=V):
+            nc.vector.scalar_tensor_tensor(
+                out=ubuf[i][:, lo:hi], in0=q1t[i][:, lo:hi], scalar=nsig[i][:], in1=ebuf[i][:, lo:hi],
+                op0=ALU.mult, op1=ALU.add,
+            )
+
+        def relu1(i):
+            for c, cols in chunks():
+                nc.scalar.activation(
+                    out=ebuf[i][:, cols], in_=ubuf[i][:, cols], func=ACT.Relu, accum_out=racc[i][:, c : c + 1]
+                )
+            mean(nm1[i], racc[i], -1.0)
+
+        def sub2(i, lo=0, hi=V):
+            nc.vector.scalar_tensor_tensor(
+                out=ubuf[i][:, lo:hi], in0=q2t[i][:, lo:hi], scalar=nm1[i][:], in1=ebuf[i][:, lo:hi],
+                op0=ALU.mult, op1=ALU.add,
+            )
+
+        def relu2(i, lo=0, hi=V, eng="s", c=0):
+            if eng == "s":
+                nc.scalar.activation(
+                    out=ebuf[i][:, lo:hi], in_=ubuf[i][:, lo:hi], func=ACT.Relu, accum_out=tacc[i][:, c : c + 1]
+                )
+            else:
+                nc.vector.tensor_scalar(
+                    out=ebuf[i][:, lo:hi], in0=ubuf[i][:, lo:hi], scalar1=0.0, scalar2=0.0,
+                    op0=ALU.max, op1=ALU.add, accum_out=tacc[i][:, c : c + 1],
+                )
+
+        def mean2(i):
+            mean(m2[i], tacc[i], 1.0)
+
+        def recip(i):
+            nc.vector.reciprocal(out=inv[i][:], in_=m2[i][:])
+
+        def gain(i, s, k):
+            cols = slice(512 * s, 512 * (s + k))
+            nc.vector.scalar_tensor_tensor(
+                out=cbuf[i][:, cols], in0=ebuf[i][:, cols], scalar=inv[i][:], in1=gt[:, cols],
+                op0=ALU.mult, op1=ALU.mult,
+            )
+
+        cbank = {}
+
+        def c_turn(i, s, k):
+            b = bank("turn")
+            cbank[i, s] = b
+            turn(twisted(b, k), cbuf[i][:].bitcast(F32)[:, 256 * s : 256 * (s + k)], k)
+
+        def c_copy(i, s, k, eng="s"):
+            dst = untwist(cg[i][:, 512 * s : 512 * (s + k)], k)
+            src = twisted(cbank[i, s], k).rearrange("p s u r -> p s r u")
+            if eng == "v":
+                nc.vector.tensor_copy(out=dst, in_=src)
+            else:
+                nc.scalar.copy(out=dst, in_=src)
+
+        def c_quant(i, s, k):
+            nc.vector.quantize_mx(
+                out=cc[i][:, P * s : P * (s + k)].bitcast(A4),
+                scales=ccs[i][:, P * s : P * (s + k)],
+                in_=cg[i][:, 512 * s : 512 * (s + k)],
+            )
+
+        obank = {}
+
+        def product(i, s0, k):
+            if s0 == 0:
+                obank[i, 0] = bank("acc" if i in (0, 3) else "lt")
+                obank[i, 1] = bank("acc" if i in (0, 3) else "lt")
+            for n in range(2):
+                for s in range(s0, s0 + k):
+                    nc.tensor.matmul_mx(
+                        out=obank[i, n][:],
+                        lhsT=cc[i][:, P * s : P * (s + 1)].bitcast(A4),
+                        lhsT_scale=ccs[i][:, P * s : P * (s + 1)],
+                        rhs=ew[:, s, 1024 * n : 1024 * (n + 1)].bitcast(W4),
+                        rhs_scale=es[:, s, 512 * n : 512 * (n + 1)],
+                        start=(s == 0),
+                        stop=(s == 3),
+                    )
+
+        def leave(i, n, eng):
+            cols = slice(512 * n, 512 * (n + 1))
+            if eng == "v":
+                nc.vector.tensor_copy(out=ot[i][:, cols], in_=obank[i, n][:])
+            else:
+                nc.scalar.copy(out=ot[i][:, cols], in_=obank[i, n][:])
+
+        def store(i):
+            nc.sync.dma_start(out=out[P * i : P * (i + 1), :], in_=ot[i][:])
+
+        widen(0, (3,), "s")
+        widen(0, (0, 1, 2,), "v")
+        h_turn(0, 0, 1)
+        widen(0, (7, 6,), "s")
+        widen(1, (0, 1, 2,), "v")
+        widen(1, (4, 5,), "s")
+        widen(1, (3, 7, 6,), "v")
+        h_turn(1, 0, 2)
+        widen(0, (4, 5,), "s")
+        h_copy(0, 0, 1, "v")
+        h_quant(0, 0, 1)
+        h_turn(0, 1, 1)
+        h_copy(0, 1, 1, "v")
+        h_quant(0, 1, 1)
+        lt(0)
+        h_copy(1, 0, 2, "s")
+        h_quant(1, 0, 2)
+        lt(1, (0, 1))
+        widen(2, (0, 1, 2, 3, 4, 5, 6, 7,), "s")
+        h_turn(2, 0, 2)
+        rowmax(0, (0,))
+        rowmax(0, (1, 2, 3))
+        negmax(0)
+        rowmax(1, (0, 1))
+        h_copy(2, 0, 2, "v")
+        widen(3, (0, 1, 2, 3, 4, 5, 6, 7,), "s")
+        lt(1, (2, 3))
+        exps(0)
+        h_turn(3, 0, 2)
+        h_copy(3, 0, 2, "s")
+        rowmax(1, (2, 3))
+        h_quant(2, 0, 2)
+        negmax(1)
+        exps(1)
+        sub1(0)
+        relu1(0)
+        lt(2)
+        rowmax(2)
+        h_quant(3, 0, 2)
+        negmax(2)
+        exps(2)
+        sub1(1)
+        relu1(1)
+        sub2(0)
+        relu2(0)
+        lt(3)
+        rowmax(3)
+        mean2(0)
+        sub1(2, 1024, 2048)
+        negmax(3)
+        exps(3)
+        sub1(2, 0, 1024)
+        recip(0)
+        sub2(1)
+        relu1(2)
+        gain(0, 0, 2)
+        c_turn(0, 0, 2)
+        gain(0, 2, 2)
+        relu2(1)
+        mean2(1)
+        sub2(2)
+        c_copy(0, 0, 2, "s")
+        sub1(3)
+        recip(1)
+        relu2(2)
+        c_quant(0, 0, 2)
+        c_turn(0, 2, 2)
+        c_copy(0, 2, 2, "s")
+        gain(1, 0, 2)
+        c_quant(0, 2, 2)
+        product(0, 0, 2)
+        mean2(2)
+        relu1(3)
+        product(0, 2, 2)
+        recip(2)
+        c_turn(1, 0, 2)
+        gain(1, 2, 2)
+        c_copy(1, 0, 2, "s")
+        gain(2, 0, 2)
+        gain(2, 2, 2)
+        c_turn(1, 2, 2)
+        c_copy(1, 2, 2, "s")
+        leave(0, 1, "s")
+        c_turn(2, 0, 2)
+        c_copy(2, 0, 2, "s")
+        c_quant(1, 0, 2)
+        c_turn(2, 2, 2)
+        c_copy(2, 2, 2, "s")
+        sub2(3, 0, 1024)
+        relu2(3, 0, 1024, "s", 0)
+        c_quant(1, 2, 2)
+        sub2(3, 1024, 2048)
+        relu2(3, 1024, 2048, "s", 1)
+        product(1, 0, 2)
+        product(1, 2, 2)
+        c_quant(2, 0, 2)
+        c_quant(2, 2, 2)
+        leave(1, 0, "v")
+        mean2(3)
+        product(2, 0, 2)
+        product(2, 2, 2)
+        recip(3)
+        gain(3, 0, 1)
+        gain(3, 1, 1)
+        leave(1, 1, "s")
+        c_turn(3, 0, 1)
+        c_turn(3, 1, 1)
+        gain(3, 2, 1)
+        c_turn(3, 2, 1)
+        leave(0, 0, "s")
+        c_copy(3, 0, 1, "s")
+        c_quant(3, 0, 1)
+        product(3, 0, 1)
+        gain(3, 3, 1)
+        c_copy(3, 1, 1, "s")
+        leave(2, 1, "s")
+        c_turn(3, 3, 1)
+        c_quant(3, 1, 1)
+        c_copy(3, 2, 1, "s")
+        c_quant(3, 2, 1)
+        store(1)
+        product(3, 1, 1)
+        product(3, 2, 1)
+        c_copy(3, 3, 1, "v")
+        leave(2, 0, "s")
+        c_quant(3, 3, 1)
+        product(3, 3, 1)
+        store(0)
+        store(2)
+        leave(3, 0, "s")
+        nc.sync.dma_start(out=out[P * 3 :, 0:512], in_=ot[3][:, 0:512])
+        leave(3, 1, "v")
+        nc.sync.dma_start(out=out[P * 3 :, 512:1024], in_=ot[3][:, 512:1024])

@@ -60,24 +60,25 @@ def tile_specinferrecursiveresidualverify_d2p_kernel(
         nm = [keep.tile([P, 1], F32, name="nm%d" % i) for i in range(TILES)]
         inv = [keep.tile([P, 1], F32, name="inv%d" % i) for i in range(TILES)]
         eacc = [keep.tile([P, 4], F32, name="eacc%d" % i) for i in range(TILES)]
-        racc = [keep.tile([P, CH], F32, name="racc%d" % i) for i in range(TILES)]
-        tacc = [keep.tile([P, 1 if i < 3 else 2], F32, name="tacc%d" % i) for i in range(TILES)]
+        racc = [keep.tile([P, 2], F32, name="racc%d" % i) for i in range(TILES)]
+        tacc = [keep.tile([P, 2], F32, name="tacc%d" % i) for i in range(TILES)]
         nsig = [keep.tile([P, 1], F32, name="nsig%d" % i) for i in range(TILES)]
         nm1 = [keep.tile([P, 1], F32, name="nm1%d" % i) for i in range(TILES)]
         m2 = [keep.tile([P, 1], F32, name="m2%d" % i) for i in range(TILES)]
         junk = keep.tile([P, 4], F32, name="junk")
         warm = keep.tile([P, 1], F32, name="warm")
+        zeros = keep.tile([P, 512], BF16, name="zeros")
 
         nc.scalar.dma_start(out=hs[:], in_=h_t_scale.rearrange("i j -> (i j)").partition_broadcast(P))
-        nc.vector.memset(warm[:], 0.0)
-        nc.scalar.activation(out=warm[:], in_=warm[:], func=ACT.Exp)
         nc.vector.memset(ws[:].rearrange("p g n -> p (g n)").bitcast(I32), 0)
+        nc.vector.memset(warm[:], 0.0)
+        nc.vector.memset(zeros[:], 0.0)
         make_identity(nc, ident[:])
         nc.gpsimd.memset(es[:].rearrange("p g n -> p (g n)").bitcast(I32), 0)
 
-        def load_scales(dst, src):
+        def load_scales(dst, src, queue):
             for quad in range(4):
-                nc.sync.dma_start(
+                queue.dma_start(
                     out=dst[32 * quad : 32 * quad + 4, :, :].bitcast(I32),
                     in_=src[:, 4 * quad : 4 * quad + 4, :].rearrange("g r n -> r g n").bitcast(I32),
                 )
@@ -94,25 +95,31 @@ def tile_specinferrecursiveresidualverify_d2p_kernel(
             nc.sync.dma_start(out=ww[b][:], in_=wsrc[:, :, 1024 * b : 1024 * (b + 1)])
 
         load_h(0)
-        load_h(1)
-        load_scales(ws, w_t_scales)
+        load_scales(ws, w_t_scales, nc.scalar)
+        nc.scalar.activation(out=warm[:], in_=warm[:], func=ACT.Exp)
         load_w(0)
         load_w(1)
-        load_h(2)
+        load_h(1)
         load_w(2)
         load_w(3)
+        load_h(2)
         load_h(3)
         load_q(q1t, q1, 0)
         load_q(q1t, q1, 1)
         load_q(q2t, q2, 0)
         load_q(q1t, q1, 2)
         load_q(q2t, q2, 1)
-        nc.sync.dma_start(out=gt[:], in_=g.partition_broadcast(P))
         load_q(q1t, q1, 3)
         load_q(q2t, q2, 2)
-        load_scales(es, emb_scales)
+        load_scales(es, emb_scales, nc.sync)
         nc.sync.dma_start(out=ew[:], in_=emb_words.rearrange("g p c -> p g c"))
         load_q(q2t, q2, 3)
+        nc.sync.dma_start(out=gt[:], in_=g.partition_broadcast(P))
+
+        def dummy(n, use):
+            b = bank(use)
+            for k in range(n):
+                nc.tensor.matmul(out=b[:], lhsT=zeros[:, :P], rhs=zeros[:], start=True, stop=True)
 
         def widen(i, blocks, eng):
             for j in blocks:
@@ -210,11 +217,13 @@ def tile_specinferrecursiveresidualverify_d2p_kernel(
                 op0=ALU.mult, op1=ALU.add,
             )
 
-        def relu1(i):
-            for c, cols in chunks():
-                nc.scalar.activation(
-                    out=ebuf[i][:, cols], in_=ubuf[i][:, cols], func=ACT.Relu, accum_out=racc[i][:, c : c + 1]
-                )
+        def relu1(i, c):
+            lo, hi = 1024 * c, 1024 * (c + 1)
+            nc.scalar.activation(
+                out=ebuf[i][:, lo:hi], in_=ubuf[i][:, lo:hi], func=ACT.Relu, accum_out=racc[i][:, c : c + 1]
+            )
+
+        def mean1(i):
             mean(nm1[i], racc[i], -1.0)
 
         def sub2(i, lo=0, hi=V):
@@ -297,136 +306,201 @@ def tile_specinferrecursiveresidualverify_d2p_kernel(
         def store(i):
             nc.sync.dma_start(out=out[P * i : P * (i + 1), :], in_=ot[i][:])
 
-        widen(0, (3,), "s")
-        widen(0, (0, 1, 2,), "v")
+        widen(0, (3,), "v")
+        widen(0, (2,), "v")
+        widen(0, (1,), "v")
+        widen(0, (0,), "s")
+        widen(0, (4,), "v")
+        widen(0, (5,), "s")
+        widen(0, (6,), "s")
         h_turn(0, 0, 1)
-        widen(0, (7, 6,), "s")
-        widen(1, (0, 1, 2,), "v")
-        widen(1, (4, 5,), "s")
-        widen(1, (3, 7, 6,), "v")
-        h_turn(1, 0, 2)
-        widen(0, (4, 5,), "s")
+        widen(0, (7,), "v")
         h_copy(0, 0, 1, "v")
-        h_quant(0, 0, 1)
         h_turn(0, 1, 1)
-        h_copy(0, 1, 1, "v")
+        dummy(1, "lt")
+        h_quant(0, 0, 1)
+        h_copy(0, 1, 1, "s")
         h_quant(0, 1, 1)
-        lt(0)
+        widen(1, (3,), "v")
+        widen(1, (1,), "s")
+        lt(0, (0,))
+        widen(1, (2,), "s")
+        widen(1, (7,), "s")
+        lt(0, (1,))
+        widen(1, (0,), "v")
+        widen(1, (5,), "s")
+        widen(1, (6,), "v")
+        widen(1, (4,), "v")
+        h_turn(1, 0, 2)
         h_copy(1, 0, 2, "s")
-        h_quant(1, 0, 2)
-        lt(1, (0, 1))
-        widen(2, (0, 1, 2, 3, 4, 5, 6, 7,), "s")
-        h_turn(2, 0, 2)
+        widen(2, (2,), "s")
         rowmax(0, (0,))
-        rowmax(0, (1, 2, 3))
+        widen(2, (3,), "s")
+        lt(0, (3,))
+        rowmax(0, (1,))
+        widen(2, (4,), "v")
+        widen(2, (5,), "s")
+        widen(2, (0,), "v")
+        widen(2, (7,), "s")
+        lt(0, (2,))
+        widen(2, (6,), "v")
+        widen(2, (1,), "v")
+        dummy(0, "acc")
+        h_turn(2, 0, 2)
+        widen(3, (5,), "v")
+        rowmax(0, (3,))
+        h_quant(1, 0, 2)
+        widen(3, (1,), "s")
+        widen(3, (3,), "s")
+        lt(1, (0,))
+        widen(3, (2,), "s")
+        rowmax(0, (2,))
         negmax(0)
-        rowmax(1, (0, 1))
-        h_copy(2, 0, 2, "v")
-        widen(3, (0, 1, 2, 3, 4, 5, 6, 7,), "s")
-        lt(1, (2, 3))
-        exps(0)
+        widen(3, (4,), "v")
+        lt(1, (1,))
+        lt(1, (2,))
+        widen(3, (7,), "s")
+        lt(1, (3,))
+        widen(3, (0,), "v")
+        rowmax(1, (0,))
+        rowmax(1, (1,))
+        widen(3, (6,), "s")
         h_turn(3, 0, 2)
-        h_copy(3, 0, 2, "s")
-        rowmax(1, (2, 3))
+        dummy(1, "turn")
+        h_copy(2, 0, 2, "s")
         h_quant(2, 0, 2)
+        lt(2, (0,))
+        rowmax(1, (2,))
+        exps(0)
+        lt(2, (3,))
+        rowmax(1, (3,))
+        lt(2, (1,))
         negmax(1)
-        exps(1)
-        sub1(0)
-        relu1(0)
-        lt(2)
-        rowmax(2)
+        sub1(0, 1024, 2048)
+        sub1(0, 0, 1024)
+        rowmax(2, (0,))
+        rowmax(2, (3,))
+        rowmax(2, (1,))
+        h_copy(3, 0, 2, "s")
+        lt(2, (2,))
+        rowmax(2, (2,))
         h_quant(3, 0, 2)
+        exps(1)
         negmax(2)
+        sub1(1, 1024, 2048)
+        relu1(0, 1)
+        relu1(0, 0)
+        sub1(1, 0, 1024)
+        mean1(0)
         exps(2)
-        sub1(1)
-        relu1(1)
-        sub2(0)
-        relu2(0)
-        lt(3)
-        rowmax(3)
-        mean2(0)
+        relu1(1, 0)
+        sub2(0, 1024, 2048)
+        relu2(0, 1024, 2048, "s", 1)
+        relu1(1, 1)
+        lt(3, (2,))
+        rowmax(3, (2,))
+        sub1(2, 0, 1024)
+        sub2(0, 0, 1024)
+        relu2(0, 0, 1024, "s", 0)
+        mean1(1)
         sub1(2, 1024, 2048)
+        lt(3, (0,))
+        lt(3, (3,))
+        rowmax(3, (3,))
+        lt(3, (1,))
+        mean2(0)
+        rowmax(3, (1,))
+        relu1(2, 0)
+        rowmax(3, (0,))
+        relu1(2, 1)
+        sub2(1, 0, 1024)
         negmax(3)
         exps(3)
-        sub1(2, 0, 1024)
         recip(0)
-        sub2(1)
-        relu1(2)
-        gain(0, 0, 2)
-        c_turn(0, 0, 2)
+        sub2(1, 1024, 2048)
         gain(0, 2, 2)
-        relu2(1)
-        mean2(1)
-        sub2(2)
-        c_copy(0, 0, 2, "s")
-        sub1(3)
-        recip(1)
-        relu2(2)
-        c_quant(0, 0, 2)
+        mean1(2)
+        relu2(1, 0, 1024, "s", 0)
+        gain(0, 0, 2)
+        relu2(1, 1024, 2048, "s", 1)
+        c_turn(0, 0, 2)
         c_turn(0, 2, 2)
-        c_copy(0, 2, 2, "s")
-        gain(1, 0, 2)
-        c_quant(0, 2, 2)
-        product(0, 0, 2)
+        mean2(1)
+        c_copy(0, 0, 2, "s")
+        sub1(3, 1024, 2048)
+        sub2(2, 0, 1024)
+        relu2(2, 0, 1024, "s", 0)
+        sub2(2, 1024, 2048)
+        relu2(2, 1024, 2048, "s", 1)
         mean2(2)
-        relu1(3)
-        product(0, 2, 2)
-        recip(2)
-        c_turn(1, 0, 2)
+        recip(1)
+        c_quant(0, 0, 2)
+        dummy(5, "acc")
+        gain(1, 0, 2)
         gain(1, 2, 2)
+        c_turn(1, 0, 2)
+        c_copy(0, 2, 2, "s")
+        c_turn(1, 2, 2)
+        recip(2)
+        relu1(3, 1)
         c_copy(1, 0, 2, "s")
+        product(0, 0, 2)
+        sub1(3, 0, 1024)
+        relu1(3, 0)
+        c_quant(0, 2, 2)
+        product(0, 2, 2)
+        mean1(3)
         gain(2, 0, 2)
         gain(2, 2, 2)
-        c_turn(1, 2, 2)
-        c_copy(1, 2, 2, "s")
-        leave(0, 1, "s")
-        c_turn(2, 0, 2)
-        c_copy(2, 0, 2, "s")
         c_quant(1, 0, 2)
+        c_copy(1, 2, 2, "s")
+        c_turn(2, 0, 2)
         c_turn(2, 2, 2)
+        c_copy(2, 0, 2, "s")
         c_copy(2, 2, 2, "s")
+        sub2(3, 1024, 2048)
+        product(1, 0, 2)
+        relu2(3, 1024, 2048, "s", 1)
+        c_quant(1, 2, 2)
+        product(1, 2, 2)
         sub2(3, 0, 1024)
         relu2(3, 0, 1024, "s", 0)
-        c_quant(1, 2, 2)
-        sub2(3, 1024, 2048)
-        relu2(3, 1024, 2048, "s", 1)
-        product(1, 0, 2)
-        product(1, 2, 2)
-        c_quant(2, 0, 2)
-        c_quant(2, 2, 2)
-        leave(1, 0, "v")
         mean2(3)
+        c_quant(2, 0, 2)
+        leave(1, 0, "s")
+        c_quant(2, 2, 2)
+        recip(3)
+        leave(0, 1, "s")
         product(2, 0, 2)
         product(2, 2, 2)
-        recip(3)
         gain(3, 0, 1)
-        gain(3, 1, 1)
-        leave(1, 1, "s")
-        c_turn(3, 0, 1)
-        c_turn(3, 1, 1)
-        gain(3, 2, 1)
-        c_turn(3, 2, 1)
         leave(0, 0, "s")
+        gain(3, 1, 1)
+        c_turn(3, 0, 1)
         c_copy(3, 0, 1, "s")
+        store(0)
+        gain(3, 2, 1)
+        c_turn(3, 1, 1)
+        c_turn(3, 2, 1)
         c_quant(3, 0, 1)
         product(3, 0, 1)
+        leave(1, 1, "s")
         gain(3, 3, 1)
-        c_copy(3, 1, 1, "s")
-        leave(2, 1, "s")
-        c_turn(3, 3, 1)
-        c_quant(3, 1, 1)
-        c_copy(3, 2, 1, "s")
-        c_quant(3, 2, 1)
         store(1)
+        c_turn(3, 3, 1)
+        c_copy(3, 1, 1, "s")
+        c_quant(3, 1, 1)
         product(3, 1, 1)
+        c_copy(3, 2, 1, "v")
+        c_quant(3, 2, 1)
+        leave(2, 1, "s")
         product(3, 2, 1)
-        c_copy(3, 3, 1, "v")
         leave(2, 0, "s")
+        store(2)
+        c_copy(3, 3, 1, "v")
         c_quant(3, 3, 1)
         product(3, 3, 1)
-        store(0)
-        store(2)
-        leave(3, 0, "s")
+        leave(3, 0, "v")
+        leave(3, 1, "s")
         nc.sync.dma_start(out=out[P * 3 :, 0:512], in_=ot[3][:, 0:512])
-        leave(3, 1, "v")
         nc.sync.dma_start(out=out[P * 3 :, 512:1024], in_=ot[3][:, 512:1024])

@@ -35,7 +35,9 @@ def tile_specinferrecursiveresidualverify_d2p_kernel(
         def bank(use):
             return psum.tile([P, 512], F32, name=use, tag=use, bufs=4 if use == "lt" else 2)
 
-        hb = [keep.tile([P, D], U8, name="hb%d" % i, align_bytes=64) for i in range(TILES)]
+        hb0 = keep.tile([P, D], U8, name="hb0", align_bytes=64)
+        hbr = keep.tile([P, TILES - 1, D], U8, name="hbr", align_bytes=64)
+        hb = [hb0] + [hbr[:, i, :] for i in range(TILES - 1)]
         hs = keep.tile([P, 32], F32, name="hs")
         hw = [keep.tile([P, D], BF16, name="hw%d" % i, align_bytes=64) for i in range(TILES)]
         hg = [keep.tile([P, 1024], BF16, name="hg%d" % i, align_bytes=64) for i in range(TILES)]
@@ -60,8 +62,8 @@ def tile_specinferrecursiveresidualverify_d2p_kernel(
         nm = [keep.tile([P, 1], F32, name="nm%d" % i) for i in range(TILES)]
         inv = [keep.tile([P, 1], F32, name="inv%d" % i) for i in range(TILES)]
         eacc = [keep.tile([P, 4], F32, name="eacc%d" % i) for i in range(TILES)]
-        racc = [keep.tile([P, 2], F32, name="racc%d" % i) for i in range(TILES)]
-        tacc = [keep.tile([P, 2], F32, name="tacc%d" % i) for i in range(TILES)]
+        racc = [keep.tile([P, CH], F32, name="racc%d" % i) for i in range(TILES)]
+        tacc = [keep.tile([P, 1 if i < 3 else 2], F32, name="tacc%d" % i) for i in range(TILES)]
         nsig = [keep.tile([P, 1], F32, name="nsig%d" % i) for i in range(TILES)]
         nm1 = [keep.tile([P, 1], F32, name="nm1%d" % i) for i in range(TILES)]
         m2 = [keep.tile([P, 1], F32, name="m2%d" % i) for i in range(TILES)]
@@ -69,22 +71,26 @@ def tile_specinferrecursiveresidualverify_d2p_kernel(
         warm = keep.tile([P, 1], F32, name="warm")
         zeros = keep.tile([P, 512], BF16, name="zeros")
 
-        nc.scalar.dma_start(out=hs[:], in_=h_t_scale.rearrange("i j -> (i j)").partition_broadcast(P))
-        nc.vector.memset(ws[:].rearrange("p g n -> p (g n)").bitcast(I32), 0)
+        nc.sync.dma_start(out=hs[:], in_=h_t_scale.rearrange("i j -> (i j)").partition_broadcast(P))
         nc.vector.memset(warm[:], 0.0)
+        nc.scalar.activation(out=warm[:], in_=warm[:], func=ACT.Exp)
+        nc.vector.memset(ws[:].rearrange("p g n -> p (g n)").bitcast(I32), 0)
         nc.vector.memset(zeros[:], 0.0)
         make_identity(nc, ident[:])
         nc.gpsimd.memset(es[:].rearrange("p g n -> p (g n)").bitcast(I32), 0)
 
-        def load_scales(dst, src, queue):
+        def load_scales(dst, src):
             for quad in range(4):
-                queue.dma_start(
+                nc.sync.dma_start(
                     out=dst[32 * quad : 32 * quad + 4, :, :].bitcast(I32),
                     in_=src[:, 4 * quad : 4 * quad + 4, :].rearrange("g r n -> r g n").bitcast(I32),
                 )
 
         def load_h(i):
-            nc.sync.dma_start(out=hb[i][:], in_=h_t_bytes[P * i : P * (i + 1), :])
+            if i == 0:
+                nc.sync.dma_start(out=hb0[:], in_=h_t_bytes[:P, :])
+            else:
+                nc.sync.dma_start(out=hbr[:], in_=h_t_bytes[P:, :].rearrange("(i p) k -> p i k", p=P))
 
         def load_q(dst, src, i):
             nc.sync.dma_start(out=dst[i][:], in_=src[P * i : P * (i + 1), :])
@@ -95,15 +101,12 @@ def tile_specinferrecursiveresidualverify_d2p_kernel(
             nc.sync.dma_start(out=ww[b][:], in_=wsrc[:, :, 1024 * b : 1024 * (b + 1)])
 
         load_h(0)
-        load_scales(ws, w_t_scales, nc.scalar)
-        nc.scalar.activation(out=warm[:], in_=warm[:], func=ACT.Exp)
+        load_h(1)
+        load_scales(ws, w_t_scales)
         load_w(0)
         load_w(1)
-        load_h(1)
         load_w(2)
         load_w(3)
-        load_h(2)
-        load_h(3)
         load_q(q1t, q1, 0)
         load_q(q1t, q1, 1)
         load_q(q2t, q2, 0)
@@ -111,7 +114,7 @@ def tile_specinferrecursiveresidualverify_d2p_kernel(
         load_q(q2t, q2, 1)
         load_q(q1t, q1, 3)
         load_q(q2t, q2, 2)
-        load_scales(es, emb_scales, nc.sync)
+        load_scales(es, emb_scales)
         nc.sync.dma_start(out=ew[:], in_=emb_words.rearrange("g p c -> p g c"))
         load_q(q2t, q2, 3)
         nc.sync.dma_start(out=gt[:], in_=g.partition_broadcast(P))
@@ -191,9 +194,12 @@ def tile_specinferrecursiveresidualverify_d2p_kernel(
 
         def mean(dst, acc, sign):
             n = acc.shape[1]
-            nc.scalar.activation(
-                out=junk[:, :n], in_=acc[:], func=ACT.Copy, scale=sign / V, accum_out=dst[:]
-            )
+            if n == 1:
+                nc.scalar.activation(out=dst[:], in_=acc[:], func=ACT.Copy, scale=sign / V)
+            else:
+                nc.scalar.activation(
+                    out=junk[:, :n], in_=acc[:], func=ACT.Copy, scale=sign / V, accum_out=dst[:]
+                )
 
         def exps(i):
             for b in range(4):
@@ -217,13 +223,11 @@ def tile_specinferrecursiveresidualverify_d2p_kernel(
                 op0=ALU.mult, op1=ALU.add,
             )
 
-        def relu1(i, c):
-            lo, hi = 1024 * c, 1024 * (c + 1)
-            nc.scalar.activation(
-                out=ebuf[i][:, lo:hi], in_=ubuf[i][:, lo:hi], func=ACT.Relu, accum_out=racc[i][:, c : c + 1]
-            )
-
-        def mean1(i):
+        def relu1(i):
+            for c, cols in chunks():
+                nc.scalar.activation(
+                    out=ebuf[i][:, cols], in_=ubuf[i][:, cols], func=ACT.Relu, accum_out=racc[i][:, c : c + 1]
+                )
             mean(nm1[i], racc[i], -1.0)
 
         def sub2(i, lo=0, hi=V):
@@ -307,200 +311,179 @@ def tile_specinferrecursiveresidualverify_d2p_kernel(
             nc.sync.dma_start(out=out[P * i : P * (i + 1), :], in_=ot[i][:])
 
         widen(0, (3,), "v")
-        widen(0, (2,), "v")
         widen(0, (1,), "v")
         widen(0, (0,), "s")
+        widen(0, (2,), "s")
+        dummy(3, "acc")
         widen(0, (4,), "v")
-        widen(0, (5,), "s")
-        widen(0, (6,), "s")
+        widen(0, (7,), "s")
+        widen(0, (5,), "v")
         h_turn(0, 0, 1)
-        widen(0, (7,), "v")
+        widen(0, (6,), "v")
+        widen(1, (0,), "v")
         h_copy(0, 0, 1, "v")
+        widen(1, (6,), "s")
+        widen(1, (7,), "s")
         h_turn(0, 1, 1)
-        dummy(1, "lt")
         h_quant(0, 0, 1)
         h_copy(0, 1, 1, "s")
-        h_quant(0, 1, 1)
-        widen(1, (3,), "v")
-        widen(1, (1,), "s")
-        lt(0, (0,))
-        widen(1, (2,), "s")
-        widen(1, (7,), "s")
-        lt(0, (1,))
-        widen(1, (0,), "v")
+        dummy(2, "acc")
         widen(1, (5,), "s")
-        widen(1, (6,), "v")
+        widen(3, (6,), "v")
+        widen(2, (3,), "s")
+        h_quant(0, 1, 1)
+        widen(1, (3,), "s")
+        widen(2, (5,), "s")
+        widen(2, (7,), "v")
+        widen(1, (1,), "s")
+        widen(1, (2,), "s")
+        widen(2, (1,), "v")
+        widen(3, (1,), "s")
+        widen(3, (7,), "s")
+        widen(3, (5,), "v")
+        widen(3, (0,), "s")
+        widen(2, (2,), "s")
+        widen(2, (0,), "v")
+        lt(0, (0,))
+        lt(0, (1,))
         widen(1, (4,), "v")
         h_turn(1, 0, 2)
-        h_copy(1, 0, 2, "s")
-        widen(2, (2,), "s")
         rowmax(0, (0,))
-        widen(2, (3,), "s")
-        lt(0, (3,))
         rowmax(0, (1,))
-        widen(2, (4,), "v")
-        widen(2, (5,), "s")
-        widen(2, (0,), "v")
-        widen(2, (7,), "s")
-        lt(0, (2,))
+        h_copy(1, 0, 2, "s")
         widen(2, (6,), "v")
-        widen(2, (1,), "v")
-        dummy(0, "acc")
-        h_turn(2, 0, 2)
-        widen(3, (5,), "v")
-        rowmax(0, (3,))
-        h_quant(1, 0, 2)
-        widen(3, (1,), "s")
         widen(3, (3,), "s")
-        lt(1, (0,))
+        lt(0, (3,))
+        widen(2, (4,), "s")
+        rowmax(0, (3,))
         widen(3, (2,), "s")
-        rowmax(0, (2,))
-        negmax(0)
-        widen(3, (4,), "v")
+        widen(3, (4,), "s")
+        h_quant(1, 0, 2)
+        lt(0, (2,))
+        h_turn(2, 0, 2)
+        h_copy(2, 0, 2, "s")
+        lt(1, (0,))
         lt(1, (1,))
-        lt(1, (2,))
-        widen(3, (7,), "s")
+        rowmax(0, (2,))
         lt(1, (3,))
-        widen(3, (0,), "v")
+        lt(1, (2,))
+        negmax(0)
         rowmax(1, (0,))
         rowmax(1, (1,))
-        widen(3, (6,), "s")
-        h_turn(3, 0, 2)
-        dummy(1, "turn")
-        h_copy(2, 0, 2, "s")
         h_quant(2, 0, 2)
-        lt(2, (0,))
-        rowmax(1, (2,))
-        exps(0)
-        lt(2, (3,))
-        rowmax(1, (3,))
         lt(2, (1,))
+        rowmax(1, (3,))
+        exps(0)
+        rowmax(1, (2,))
         negmax(1)
-        sub1(0, 1024, 2048)
-        sub1(0, 0, 1024)
+        h_turn(3, 0, 2)
+        lt(2, (2,))
+        sub1(0)
+        exps(1)
+        rowmax(2, (1,))
+        rowmax(2, (2,))
+        h_copy(3, 0, 2, "s")
+        lt(2, (0,))
+        lt(2, (3,))
         rowmax(2, (0,))
         rowmax(2, (3,))
-        rowmax(2, (1,))
-        h_copy(3, 0, 2, "s")
-        lt(2, (2,))
-        rowmax(2, (2,))
         h_quant(3, 0, 2)
-        exps(1)
         negmax(2)
-        sub1(1, 1024, 2048)
-        relu1(0, 1)
-        relu1(0, 0)
-        sub1(1, 0, 1024)
-        mean1(0)
-        exps(2)
-        relu1(1, 0)
-        sub2(0, 1024, 2048)
-        relu2(0, 1024, 2048, "s", 1)
-        relu1(1, 1)
+        lt(3, (3,))
         lt(3, (2,))
+        relu1(0)
+        sub1(1)
+        sub2(0)
+        exps(2)
+        relu1(1)
+        relu2(0)
+        mean2(0)
+        lt(3, (1,))
+        rowmax(3, (3,))
+        rowmax(3, (1,))
+        lt(3, (0,))
+        rowmax(3, (0,))
         rowmax(3, (2,))
         sub1(2, 0, 1024)
-        sub2(0, 0, 1024)
-        relu2(0, 0, 1024, "s", 0)
-        mean1(1)
-        sub1(2, 1024, 2048)
-        lt(3, (0,))
-        lt(3, (3,))
-        rowmax(3, (3,))
-        lt(3, (1,))
-        mean2(0)
-        rowmax(3, (1,))
-        relu1(2, 0)
-        rowmax(3, (0,))
-        relu1(2, 1)
-        sub2(1, 0, 1024)
         negmax(3)
-        exps(3)
+        sub1(2, 1024, 2048)
         recip(0)
-        sub2(1, 1024, 2048)
-        gain(0, 2, 2)
-        mean1(2)
-        relu2(1, 0, 1024, "s", 0)
-        gain(0, 0, 2)
-        relu2(1, 1024, 2048, "s", 1)
-        c_turn(0, 0, 2)
+        sub2(1)
+        exps(3)
+        relu1(2)
+        gain(0, 0, 4)
+        sub1(3)
+        dummy(3, "turn")
         c_turn(0, 2, 2)
+        c_turn(0, 0, 2)
+        relu2(1)
+        sub2(2)
+        c_copy(0, 2, 2, "s")
         mean2(1)
         c_copy(0, 0, 2, "s")
-        sub1(3, 1024, 2048)
-        sub2(2, 0, 1024)
-        relu2(2, 0, 1024, "s", 0)
-        sub2(2, 1024, 2048)
-        relu2(2, 1024, 2048, "s", 1)
-        mean2(2)
+        relu2(2)
         recip(1)
-        c_quant(0, 0, 2)
-        dummy(5, "acc")
-        gain(1, 0, 2)
-        gain(1, 2, 2)
-        c_turn(1, 0, 2)
-        c_copy(0, 2, 2, "s")
-        c_turn(1, 2, 2)
-        recip(2)
-        relu1(3, 1)
-        c_copy(1, 0, 2, "s")
+        c_quant(0, 0, 4)
+        mean2(2)
         product(0, 0, 2)
-        sub1(3, 0, 1024)
-        relu1(3, 0)
-        c_quant(0, 2, 2)
-        product(0, 2, 2)
-        mean1(3)
+        dummy(0, "acc")
+        gain(1, 0, 4)
+        c_turn(1, 0, 2)
+        recip(2)
         gain(2, 0, 2)
         gain(2, 2, 2)
-        c_quant(1, 0, 2)
+        relu1(3)
+        c_turn(1, 2, 2)
+        c_copy(1, 0, 2, "s")
         c_copy(1, 2, 2, "s")
-        c_turn(2, 0, 2)
-        c_turn(2, 2, 2)
-        c_copy(2, 0, 2, "s")
-        c_copy(2, 2, 2, "s")
-        sub2(3, 1024, 2048)
-        product(1, 0, 2)
-        relu2(3, 1024, 2048, "s", 1)
-        c_quant(1, 2, 2)
-        product(1, 2, 2)
         sub2(3, 0, 1024)
+        c_quant(1, 0, 4)
+        product(0, 2, 2)
+        sub2(3, 1024, 2048)
+        c_turn(2, 0, 2)
         relu2(3, 0, 1024, "s", 0)
-        mean2(3)
+        c_turn(2, 2, 2)
+        product(1, 0, 2)
+        c_copy(2, 0, 2, "s")
+        c_copy(2, 2, 2, "v")
         c_quant(2, 0, 2)
-        leave(1, 0, "s")
+        relu2(3, 1024, 2048, "s", 1)
+        mean2(3)
+        leave(0, 0, "s")
+        product(1, 2, 2)
         c_quant(2, 2, 2)
         recip(3)
-        leave(0, 1, "s")
-        product(2, 0, 2)
-        product(2, 2, 2)
         gain(3, 0, 1)
-        leave(0, 0, "s")
         gain(3, 1, 1)
+        product(2, 0, 2)
+        leave(1, 1, "s")
+        leave(0, 1, "s")
+        gain(3, 2, 1)
+        gain(3, 3, 1)
+        product(2, 2, 2)
         c_turn(3, 0, 1)
         c_copy(3, 0, 1, "s")
-        store(0)
-        gain(3, 2, 1)
         c_turn(3, 1, 1)
-        c_turn(3, 2, 1)
         c_quant(3, 0, 1)
-        product(3, 0, 1)
-        leave(1, 1, "s")
-        gain(3, 3, 1)
-        store(1)
-        c_turn(3, 3, 1)
+        c_turn(3, 2, 1)
         c_copy(3, 1, 1, "s")
+        c_turn(3, 3, 1)
         c_quant(3, 1, 1)
-        product(3, 1, 1)
-        c_copy(3, 2, 1, "v")
+        leave(1, 0, "s")
+        c_copy(3, 2, 1, "s")
+        product(3, 0, 1)
+        leave(2, 1, "v")
         c_quant(3, 2, 1)
-        leave(2, 1, "s")
+        product(3, 1, 1)
+        store(0)
+        c_copy(3, 3, 1, "v")
+        store(1)
+        c_quant(3, 3, 1)
         product(3, 2, 1)
+        product(3, 3, 1)
         leave(2, 0, "s")
         store(2)
-        c_copy(3, 3, 1, "v")
-        c_quant(3, 3, 1)
-        product(3, 3, 1)
-        leave(3, 0, "v")
-        leave(3, 1, "s")
+        leave(3, 0, "s")
         nc.sync.dma_start(out=out[P * 3 :, 0:512], in_=ot[3][:, 0:512])
+        leave(3, 1, "s")
         nc.sync.dma_start(out=out[P * 3 :, 512:1024], in_=ot[3][:, 512:1024])

@@ -172,7 +172,7 @@ def tile_specinferrecursiveresidualverify_d2p_kernel(
 
         def lt(i, banks=range(4)):
             for b in banks:
-                t = bank("acc" if i == 1 and b < 2 else "lt")
+                t = bank("lt" if i != 1 else "acc" if b < 2 else "turn")
                 ltb[i, b] = t
                 for s in range(2):
                     nc.tensor.matmul_mx(
@@ -310,180 +310,178 @@ def tile_specinferrecursiveresidualverify_d2p_kernel(
         def store(i):
             nc.sync.dma_start(out=out[P * i : P * (i + 1), :], in_=ot[i][:])
 
-        widen(0, (3,), "v")
-        widen(0, (1,), "v")
-        widen(0, (0,), "s")
+        widen(0, (1,), "s")
         widen(0, (2,), "s")
+        widen(0, (0,), "v")
         dummy(3, "acc")
-        widen(0, (4,), "v")
-        widen(0, (7,), "s")
-        widen(0, (5,), "v")
-        h_turn(0, 0, 1)
-        widen(0, (6,), "v")
-        widen(1, (0,), "v")
-        h_copy(0, 0, 1, "v")
-        widen(1, (6,), "s")
-        widen(1, (7,), "s")
-        h_turn(0, 1, 1)
-        h_quant(0, 0, 1)
-        h_copy(0, 1, 1, "s")
-        dummy(2, "acc")
-        widen(1, (5,), "s")
-        widen(3, (6,), "v")
-        widen(2, (3,), "s")
-        h_quant(0, 1, 1)
-        widen(1, (3,), "s")
-        widen(2, (5,), "s")
-        widen(2, (7,), "v")
-        widen(1, (1,), "s")
+        widen(0, (6,), "s")
         widen(1, (2,), "s")
-        widen(2, (1,), "v")
-        widen(3, (1,), "s")
-        widen(3, (7,), "s")
-        widen(3, (5,), "v")
-        widen(3, (0,), "s")
-        widen(2, (2,), "s")
-        widen(2, (0,), "v")
-        lt(0, (0,))
-        lt(0, (1,))
+        widen(0, (4,), "v")
+        widen(1, (5,), "s")
+        widen(0, (3,), "v")
+        h_turn(0, 0, 1)
+        widen(0, (5,), "v")
+        widen(0, (7,), "v")
+        h_turn(0, 1, 1)
+        h_copy(0, 0, 1, "s")
+        dummy(2, "acc")
+        h_copy(0, 1, 1, "s")
+        widen(2, (6,), "s")
+        widen(2, (7,), "s")
+        widen(3, (4,), "v")
+        widen(2, (5,), "s")
+        widen(3, (5,), "s")
+        widen(1, (3,), "v")
+        widen(1, (0,), "v")
+        widen(1, (1,), "v")
+        widen(1, (7,), "v")
+        widen(1, (6,), "v")
         widen(1, (4,), "v")
         h_turn(1, 0, 2)
-        rowmax(0, (0,))
-        rowmax(0, (1,))
-        h_copy(1, 0, 2, "s")
-        widen(2, (6,), "v")
-        widen(3, (3,), "s")
-        lt(0, (3,))
-        widen(2, (4,), "s")
-        rowmax(0, (3,))
+        h_quant(0, 0, 1)
+        h_quant(0, 1, 1)
+        lt(0, (0,))
+        widen(2, (0,), "v")
         widen(3, (2,), "s")
-        widen(3, (4,), "s")
-        h_quant(1, 0, 2)
+        widen(3, (0,), "s")
+        widen(2, (1,), "s")
+        widen(2, (3,), "s")
+        widen(3, (1,), "v")
+        widen(2, (2,), "s")
+        h_copy(1, 0, 2, "s")
+        lt(0, (1,))
+        widen(3, (3,), "v")
+        widen(2, (4,), "s")
+        widen(3, (6,), "s")
+        widen(3, (7,), "v")
         lt(0, (2,))
+        rowmax(0, (0,))
+        lt(0, (3,))
         h_turn(2, 0, 2)
         h_copy(2, 0, 2, "s")
-        lt(1, (0,))
-        lt(1, (1,))
+        rowmax(0, (1,))
+        h_turn(3, 0, 2)
         rowmax(0, (2,))
+        h_copy(3, 0, 2, "s")
+        h_quant(1, 0, 2)
+        rowmax(0, (3,))
+        lt(1, (1,))
+        negmax(0)
+        h_quant(2, 0, 2)
+        lt(1, (0,))
+        rowmax(1, (1,))
         lt(1, (3,))
         lt(1, (2,))
-        negmax(0)
+        lt(2, (3,))
         rowmax(1, (0,))
-        rowmax(1, (1,))
-        h_quant(2, 0, 2)
-        lt(2, (1,))
         rowmax(1, (3,))
         exps(0)
         rowmax(1, (2,))
-        negmax(1)
-        h_turn(3, 0, 2)
-        lt(2, (2,))
-        sub1(0)
-        exps(1)
-        rowmax(2, (1,))
-        rowmax(2, (2,))
-        h_copy(3, 0, 2, "s")
-        lt(2, (0,))
-        lt(2, (3,))
-        rowmax(2, (0,))
         rowmax(2, (3,))
+        lt(2, (1,))
+        negmax(1)
+        sub1(0)
+        rowmax(2, (1,))
+        lt(2, (2,))
+        rowmax(2, (2,))
+        lt(2, (0,))
+        rowmax(2, (0,))
+        exps(1)
         h_quant(3, 0, 2)
         negmax(2)
-        lt(3, (3,))
-        lt(3, (2,))
         relu1(0)
-        sub1(1)
-        sub2(0)
         exps(2)
-        relu1(1)
-        relu2(0)
-        mean2(0)
-        lt(3, (1,))
-        rowmax(3, (3,))
-        rowmax(3, (1,))
-        lt(3, (0,))
-        rowmax(3, (0,))
+        sub1(1)
+        lt(3, (2,))
+        sub2(0)
+        sub1(2, 1024, 2048)
         rowmax(3, (2,))
         sub1(2, 0, 1024)
-        negmax(3)
-        sub1(2, 1024, 2048)
+        relu1(1)
+        lt(3, (0,))
+        lt(3, (3,))
+        relu2(0)
+        lt(3, (1,))
+        rowmax(3, (3,))
+        rowmax(3, (0,))
+        rowmax(3, (1,))
+        mean2(0)
         recip(0)
-        sub2(1)
-        exps(3)
         relu1(2)
+        sub2(1)
+        negmax(3)
         gain(0, 0, 4)
-        sub1(3)
-        dummy(3, "turn")
         c_turn(0, 2, 2)
         c_turn(0, 0, 2)
+        exps(3)
         relu2(1)
         sub2(2)
+        sub1(3)
         c_copy(0, 2, 2, "s")
         mean2(1)
+        recip(1)
         c_copy(0, 0, 2, "s")
         relu2(2)
-        recip(1)
         c_quant(0, 0, 4)
         mean2(2)
         product(0, 0, 2)
-        dummy(0, "acc")
         gain(1, 0, 4)
-        c_turn(1, 0, 2)
-        recip(2)
-        gain(2, 0, 2)
-        gain(2, 2, 2)
-        relu1(3)
         c_turn(1, 2, 2)
-        c_copy(1, 0, 2, "s")
+        c_turn(1, 0, 2)
+        relu1(3)
+        recip(2)
+        gain(2, 2, 2)
+        gain(2, 0, 2)
         c_copy(1, 2, 2, "s")
-        sub2(3, 0, 1024)
-        c_quant(1, 0, 4)
-        product(0, 2, 2)
         sub2(3, 1024, 2048)
-        c_turn(2, 0, 2)
-        relu2(3, 0, 1024, "s", 0)
+        product(0, 2, 2)
+        c_copy(1, 0, 2, "s")
         c_turn(2, 2, 2)
-        product(1, 0, 2)
+        c_quant(1, 0, 4)
+        c_copy(2, 2, 2, "s")
+        c_turn(2, 0, 2)
+        sub2(3, 0, 1024)
         c_copy(2, 0, 2, "s")
-        c_copy(2, 2, 2, "v")
-        c_quant(2, 0, 2)
+        product(1, 0, 2)
         relu2(3, 1024, 2048, "s", 1)
-        mean2(3)
-        leave(0, 0, "s")
         product(1, 2, 2)
+        c_quant(2, 0, 2)
+        relu2(3, 0, 1024, "s", 0)
+        mean2(3)
+        leave(1, 1, "s")
+        leave(0, 1, "v")
         c_quant(2, 2, 2)
+        leave(0, 0, "s")
         recip(3)
+        product(2, 0, 2)
+        product(2, 2, 2)
         gain(3, 0, 1)
         gain(3, 1, 1)
-        product(2, 0, 2)
-        leave(1, 1, "s")
-        leave(0, 1, "s")
-        gain(3, 2, 1)
-        gain(3, 3, 1)
-        product(2, 2, 2)
+        leave(2, 0, "s")
         c_turn(3, 0, 1)
-        c_copy(3, 0, 1, "s")
         c_turn(3, 1, 1)
-        c_quant(3, 0, 1)
-        c_turn(3, 2, 1)
+        c_copy(3, 0, 1, "s")
+        gain(3, 2, 1)
         c_copy(3, 1, 1, "s")
-        c_turn(3, 3, 1)
-        c_quant(3, 1, 1)
+        c_turn(3, 2, 1)
         leave(1, 0, "s")
         c_copy(3, 2, 1, "s")
-        product(3, 0, 1)
-        leave(2, 1, "v")
-        c_quant(3, 2, 1)
-        product(3, 1, 1)
+        gain(3, 3, 1)
+        c_quant(3, 0, 1)
         store(0)
-        c_copy(3, 3, 1, "v")
+        c_turn(3, 3, 1)
         store(1)
-        c_quant(3, 3, 1)
+        c_quant(3, 1, 1)
+        product(3, 0, 1)
+        product(3, 1, 1)
+        leave(2, 1, "v")
+        c_copy(3, 3, 1, "s")
+        c_quant(3, 2, 1)
         product(3, 2, 1)
-        product(3, 3, 1)
-        leave(2, 0, "s")
         store(2)
+        c_quant(3, 3, 1)
+        product(3, 3, 1)
         leave(3, 0, "s")
+        leave(3, 1, "v")
         nc.sync.dma_start(out=out[P * 3 :, 0:512], in_=ot[3][:, 0:512])
-        leave(3, 1, "s")
         nc.sync.dma_start(out=out[P * 3 :, 512:1024], in_=ot[3][:, 512:1024])

from contextlib import ExitStack

import concourse.mybir as mybir
from concourse.masks import make_identity

N, D, V, E = 512, 1024, 2048, 1024
FLOPS = 2 * N * D * V + 2 * N * V * E

F32 = mybir.dt.float32
BF16 = mybir.dt.bfloat16
U8 = mybir.dt.uint8
U32 = mybir.dt.uint32
I32 = mybir.dt.int32
FP8 = mybir.dt.float8_e4m3fn
A4 = mybir.dt.float8_e4m3fn_x4
W4 = mybir.dt.float4_e2m1fn_x4
ALU = mybir.AluOpType
ACT = mybir.ActivationFunctionType
AX = mybir.AxisListType

P = 128
TILES = N // P
CH = 1


def tile_specinferrecursiveresidualverify_d2p_kernel(
    tc, h_t_bytes, h_t_scale, w_t_words, w_t_scales, q1, q2, g, emb_words, emb_scales, out
):
    nc = tc.nc
    with ExitStack() as ctx:
        keep = ctx.enter_context(tc.tile_pool(name="keep", bufs=1))
        psum = ctx.enter_context(tc.psum_pool(name="psum", bufs=2))
        ctx.enter_context(tc.manual_schedule())

        def bank(use):
            return psum.tile([P, 512], F32, name=use, tag=use, bufs=4 if use == "lt" else 2)

        hb0 = keep.tile([P, D], U8, name="hb0", align_bytes=64)
        hbr = keep.tile([P, TILES - 1, D], U8, name="hbr", align_bytes=64)
        hb = [hb0] + [hbr[:, i, :] for i in range(TILES - 1)]
        hs = keep.tile([P, 32], F32, name="hs")
        hw = [keep.tile([P, D], BF16, name="hw%d" % i, align_bytes=64) for i in range(TILES)]
        hg = [keep.tile([P, 1024], BF16, name="hg%d" % i, align_bytes=64) for i in range(TILES)]
        hc = [keep.tile([P, 256], U32, name="hc%d" % i, align_bytes=64) for i in range(TILES)]
        hcs = [keep.tile([P, 256], U8, name="hcs%d" % i, align_bytes=64) for i in range(TILES)]
        ww = [keep.tile([P, 2, 1024], U8, name="ww%d" % b, align_bytes=64) for b in range(4)]
        ws = keep.tile([P, 2, V], U8, name="ws", align_bytes=64)
        ew = keep.tile([P, 4, 2 * E], U8, name="ew", align_bytes=64)
        es = keep.tile([P, 4, E], U8, name="es", align_bytes=64)
        q1t = [keep.tile([P, V], BF16, name="q1t%d" % i) for i in range(TILES)]
        q2t = [keep.tile([P, V], BF16, name="q2t%d" % i) for i in range(TILES)]
        gt = keep.tile([P, V], BF16, name="gt")
        ident = keep.tile([P, P], F32, name="ident")
        ebuf = [keep.tile([P, V], F32, name="ebuf%d" % i) for i in range(TILES)]
        ubuf = [keep.tile([P, V], F32, name="ubuf%d" % i) for i in range(TILES)]
        cbuf = [keep.tile([P, V], BF16, name="cbuf%d" % i, align_bytes=64) for i in range(TILES)]
        cg = [keep.tile([P, 2048], BF16, name="cg%d" % i, align_bytes=64) for i in range(TILES)]
        cc = [keep.tile([P, 512], U32, name="cc%d" % i, align_bytes=64) for i in range(TILES)]
        ccs = [keep.tile([P, 512], U8, name="ccs%d" % i, align_bytes=64) for i in range(TILES)]
        ot = [keep.tile([P, E], F32, name="ot%d" % i) for i in range(TILES)]
        mx = [keep.tile([P, 4], F32, name="mx%d" % i) for i in range(TILES)]
        nm = [keep.tile([P, 1], F32, name="nm%d" % i) for i in range(TILES)]
        inv = [keep.tile([P, 1], F32, name="inv%d" % i) for i in range(TILES)]
        eacc = [keep.tile([P, 4], F32, name="eacc%d" % i) for i in range(TILES)]
        racc = [keep.tile([P, CH], F32, name="racc%d" % i) for i in range(TILES)]
        tacc = [keep.tile([P, 1 if i < 3 else 2], F32, name="tacc%d" % i) for i in range(TILES)]
        nsig = [keep.tile([P, 1], F32, name="nsig%d" % i) for i in range(TILES)]
        nm1 = [keep.tile([P, 1], F32, name="nm1%d" % i) for i in range(TILES)]
        m2 = [keep.tile([P, 1], F32, name="m2%d" % i) for i in range(TILES)]
        junk = keep.tile([P, 4], F32, name="junk")
        warm = keep.tile([P, 1], F32, name="warm")
        zeros = keep.tile([P, 512], BF16, name="zeros")

        nc.sync.dma_start(out=hs[:], in_=h_t_scale.rearrange("i j -> (i j)").partition_broadcast(P))
        nc.vector.memset(warm[:], 0.0)
        nc.scalar.activation(out=warm[:], in_=warm[:], func=ACT.Exp)
        nc.vector.memset(ws[:].rearrange("p g n -> p (g n)").bitcast(I32), 0)
        nc.vector.memset(zeros[:], 0.0)
        make_identity(nc, ident[:])
        nc.gpsimd.memset(es[:].rearrange("p g n -> p (g n)").bitcast(I32), 0)

        def load_scales(dst, src):
            for quad in range(4):
                nc.sync.dma_start(
                    out=dst[32 * quad : 32 * quad + 4, :, :].bitcast(I32),
                    in_=src[:, 4 * quad : 4 * quad + 4, :].rearrange("g r n -> r g n").bitcast(I32),
                )

        def load_h(i):
            if i == 0:
                nc.sync.dma_start(out=hb0[:], in_=h_t_bytes[:P, :])
            else:
                nc.sync.dma_start(out=hbr[:], in_=h_t_bytes[P:, :].rearrange("(i p) k -> p i k", p=P))

        def load_q(dst, src, i):
            nc.sync.dma_start(out=dst[i][:], in_=src[P * i : P * (i + 1), :])

        wsrc = w_t_words.rearrange("g p c -> p g c")

        def load_w(b):
            nc.sync.dma_start(out=ww[b][:], in_=wsrc[:, :, 1024 * b : 1024 * (b + 1)])

        load_h(0)
        load_h(1)
        load_scales(ws, w_t_scales)
        load_w(0)
        load_w(1)
        load_w(2)
        load_w(3)
        load_q(q1t, q1, 0)
        load_q(q1t, q1, 1)
        load_q(q2t, q2, 0)
        load_q(q1t, q1, 2)
        load_q(q2t, q2, 1)
        load_q(q1t, q1, 3)
        load_q(q2t, q2, 2)
        load_scales(es, emb_scales)
        nc.sync.dma_start(out=ew[:], in_=emb_words.rearrange("g p c -> p g c"))
        load_q(q2t, q2, 3)
        nc.sync.dma_start(out=gt[:], in_=g.partition_broadcast(P))

        def dummy(n, use):
            b = bank(use)
            for k in range(n):
                nc.tensor.matmul(out=b[:], lhsT=zeros[:, :P], rhs=zeros[:], start=True, stop=True)

        def widen(i, blocks, eng):
            for j in blocks:
                cols = slice(P * j, P * (j + 1))
                col = hs[:, 8 * i + j : 8 * i + j + 1]
                if eng == "v":
                    nc.vector.tensor_scalar(
                        out=hw[i][:, cols], in0=hb[i][:, cols].bitcast(FP8), scalar1=col, scalar2=None, op0=ALU.mult
                    )
                else:
                    nc.scalar.activation(out=hw[i][:, cols], in_=hb[i][:, cols].bitcast(FP8), func=ACT.Copy, scale=col)

        def turn(dst, words, k):
            for s in range(k):
                for u in range(2):
                    nc.tensor.transpose(dst[:, s, u, :], words[:, 256 * s + u : 256 * (s + 1) : 2], ident[:])

        def untwist(dst, k):
            return dst.bitcast(F32).rearrange("p (s r u) -> p s r u", s=k, u=2)

        def twisted(b, k):
            return b[:, : 256 * k].rearrange("p (s u r) -> p s u r", s=k, u=2)

        hbank = {}

        def h_turn(i, s, k):
            b = bank("turn")
            hbank[i, s] = b
            turn(twisted(b, k), hw[i][:].bitcast(F32)[:, 256 * s : 256 * (s + k)], k)

        def h_copy(i, s, k, eng):
            dst = untwist(hg[i][:, 512 * s : 512 * (s + k)], k)
            src = twisted(hbank[i, s], k).rearrange("p s u r -> p s r u")
            if eng == "v":
                nc.vector.tensor_copy(out=dst, in_=src)
            else:
                nc.scalar.copy(out=dst, in_=src)

        def h_quant(i, s, k):
            nc.vector.quantize_mx(
                out=hc[i][:, P * s : P * (s + k)].bitcast(A4),
                scales=hcs[i][:, P * s : P * (s + k)],
                in_=hg[i][:, 512 * s : 512 * (s + k)],
            )

        ltb = {}

        def lt(i, banks=range(4)):
            for b in banks:
                t = bank("lt" if i != 1 else "acc" if b < 2 else "turn")
                ltb[i, b] = t
                for s in range(2):
                    nc.tensor.matmul_mx(
                        out=t[:],
                        lhsT=hc[i][:, P * s : P * (s + 1)].bitcast(A4),
                        lhsT_scale=hcs[i][:, P * s : P * (s + 1)],
                        rhs=ww[b][:, s, :].bitcast(W4),
                        rhs_scale=ws[:, s, 512 * b : 512 * (b + 1)],
                        start=(s == 0),
                        stop=(s == 1),
                    )

        def rowmax(i, banks=range(4)):
            for b in banks:
                nc.vector.tensor_reduce(out=mx[i][:, b : b + 1], in_=ltb[i, b][:], axis=AX.X, op=ALU.max)

        def negmax(i):
            nc.vector.tensor_reduce(out=nm[i][:], in_=mx[i][:], axis=AX.X, op=ALU.max, negate=True)

        def mean(dst, acc, sign):
            n = acc.shape[1]
            if n == 1:
                nc.scalar.activation(out=dst[:], in_=acc[:], func=ACT.Copy, scale=sign / V)
            else:
                nc.scalar.activation(
                    out=junk[:, :n], in_=acc[:], func=ACT.Copy, scale=sign / V, accum_out=dst[:]
                )

        def exps(i):
            for b in range(4):
                nc.scalar.activation(
                    out=ebuf[i][:, 512 * b : 512 * (b + 1)],
                    in_=ltb[i, b][:],
                    func=ACT.Exp,
                    bias=nm[i][:],
                    scale=1.0,
                    accum_out=eacc[i][:, b : b + 1],
                )
            mean(nsig[i], eacc[i], -1.0)

        def chunks():
            w = V // CH
            return [(c, slice(w * c, w * (c + 1))) for c in range(CH)]

        def sub1(i, lo=0, hi=V):
            nc.vector.scalar_tensor_tensor(
                out=ubuf[i][:, lo:hi], in0=q1t[i][:, lo:hi], scalar=nsig[i][:], in1=ebuf[i][:, lo:hi],
                op0=ALU.mult, op1=ALU.add,
            )

        def relu1(i):
            for c, cols in chunks():
                nc.scalar.activation(
                    out=ebuf[i][:, cols], in_=ubuf[i][:, cols], func=ACT.Relu, accum_out=racc[i][:, c : c + 1]
                )
            mean(nm1[i], racc[i], -1.0)

        def sub2(i, lo=0, hi=V):
            nc.vector.scalar_tensor_tensor(
                out=ubuf[i][:, lo:hi], in0=q2t[i][:, lo:hi], scalar=nm1[i][:], in1=ebuf[i][:, lo:hi],
                op0=ALU.mult, op1=ALU.add,
            )

        def relu2(i, lo=0, hi=V, eng="s", c=0):
            if eng == "s":
                nc.scalar.activation(
                    out=ebuf[i][:, lo:hi], in_=ubuf[i][:, lo:hi], func=ACT.Relu, accum_out=tacc[i][:, c : c + 1]
                )
            else:
                nc.vector.tensor_scalar(
                    out=ebuf[i][:, lo:hi], in0=ubuf[i][:, lo:hi], scalar1=0.0, scalar2=0.0,
                    op0=ALU.max, op1=ALU.add, accum_out=tacc[i][:, c : c + 1],
                )

        def mean2(i):
            mean(m2[i], tacc[i], 1.0)

        def recip(i):
            nc.vector.reciprocal(out=inv[i][:], in_=m2[i][:])

        def gain(i, s, k):
            cols = slice(512 * s, 512 * (s + k))
            nc.vector.scalar_tensor_tensor(
                out=cbuf[i][:, cols], in0=ebuf[i][:, cols], scalar=inv[i][:], in1=gt[:, cols],
                op0=ALU.mult, op1=ALU.mult,
            )

        cbank = {}

        def c_turn(i, s, k):
            b = bank("turn")
            cbank[i, s] = b
            turn(twisted(b, k), cbuf[i][:].bitcast(F32)[:, 256 * s : 256 * (s + k)], k)

        def c_copy(i, s, k, eng="s"):
            dst = untwist(cg[i][:, 512 * s : 512 * (s + k)], k)
            src = twisted(cbank[i, s], k).rearrange("p s u r -> p s r u")
            if eng == "v":
                nc.vector.tensor_copy(out=dst, in_=src)
            else:
                nc.scalar.copy(out=dst, in_=src)

        def c_quant(i, s, k):
            nc.vector.quantize_mx(
                out=cc[i][:, P * s : P * (s + k)].bitcast(A4),
                scales=ccs[i][:, P * s : P * (s + k)],
                in_=cg[i][:, 512 * s : 512 * (s + k)],
            )

        obank = {}

        def product(i, s0, k):
            if s0 == 0:
                obank[i, 0] = bank("acc" if i in (0, 3) else "lt")
                obank[i, 1] = bank("acc" if i in (0, 3) else "lt")
            for n in range(2):
                for s in range(s0, s0 + k):
                    nc.tensor.matmul_mx(
                        out=obank[i, n][:],
                        lhsT=cc[i][:, P * s : P * (s + 1)].bitcast(A4),
                        lhsT_scale=ccs[i][:, P * s : P * (s + 1)],
                        rhs=ew[:, s, 1024 * n : 1024 * (n + 1)].bitcast(W4),
                        rhs_scale=es[:, s, 512 * n : 512 * (n + 1)],
                        start=(s == 0),
                        stop=(s == 3),
                    )

        def leave(i, n, eng):
            cols = slice(512 * n, 512 * (n + 1))
            if eng == "v":
                nc.vector.tensor_copy(out=ot[i][:, cols], in_=obank[i, n][:])
            else:
                nc.scalar.copy(out=ot[i][:, cols], in_=obank[i, n][:])

        def store(i):
            nc.sync.dma_start(out=out[P * i : P * (i + 1), :], in_=ot[i][:])

        widen(0, (1,), "s")
        widen(0, (2,), "s")
        widen(0, (0,), "v")
        dummy(3, "acc")
        widen(0, (6,), "s")
        widen(1, (2,), "s")
        widen(0, (4,), "v")
        widen(1, (5,), "s")
        widen(0, (3,), "v")
        h_turn(0, 0, 1)
        widen(0, (5,), "v")
        widen(0, (7,), "v")
        h_turn(0, 1, 1)
        h_copy(0, 0, 1, "s")
        dummy(2, "acc")
        h_copy(0, 1, 1, "s")
        widen(2, (6,), "s")
        widen(2, (7,), "s")
        widen(3, (4,), "v")
        widen(2, (5,), "s")
        widen(3, (5,), "s")
        widen(1, (3,), "v")
        widen(1, (0,), "v")
        widen(1, (1,), "v")
        widen(1, (7,), "v")
        widen(1, (6,), "v")
        widen(1, (4,), "v")
        h_turn(1, 0, 2)
        h_quant(0, 0, 1)
        h_quant(0, 1, 1)
        lt(0, (0,))
        widen(2, (0,), "v")
        widen(3, (2,), "s")
        widen(3, (0,), "s")
        widen(2, (1,), "s")
        widen(2, (3,), "s")
        widen(3, (1,), "v")
        widen(2, (2,), "s")
        h_copy(1, 0, 2, "s")
        lt(0, (1,))
        widen(3, (3,), "v")
        widen(2, (4,), "s")
        widen(3, (6,), "s")
        widen(3, (7,), "v")
        lt(0, (2,))
        rowmax(0, (0,))
        lt(0, (3,))
        h_turn(2, 0, 2)
        h_copy(2, 0, 2, "s")
        rowmax(0, (1,))
        h_turn(3, 0, 2)
        rowmax(0, (2,))
        h_copy(3, 0, 2, "s")
        h_quant(1, 0, 2)
        rowmax(0, (3,))
        lt(1, (1,))
        negmax(0)
        h_quant(2, 0, 2)
        lt(1, (0,))
        rowmax(1, (1,))
        lt(1, (3,))
        lt(1, (2,))
        lt(2, (3,))
        rowmax(1, (0,))
        rowmax(1, (3,))
        exps(0)
        rowmax(1, (2,))
        rowmax(2, (3,))
        lt(2, (1,))
        negmax(1)
        sub1(0)
        rowmax(2, (1,))
        lt(2, (2,))
        rowmax(2, (2,))
        lt(2, (0,))
        rowmax(2, (0,))
        exps(1)
        h_quant(3, 0, 2)
        negmax(2)
        relu1(0)
        exps(2)
        sub1(1)
        lt(3, (2,))
        sub2(0)
        sub1(2, 1024, 2048)
        rowmax(3, (2,))
        sub1(2, 0, 1024)
        relu1(1)
        lt(3, (0,))
        lt(3, (3,))
        relu2(0)
        lt(3, (1,))
        rowmax(3, (3,))
        rowmax(3, (0,))
        rowmax(3, (1,))
        mean2(0)
        recip(0)
        relu1(2)
        sub2(1)
        negmax(3)
        gain(0, 0, 4)
        c_turn(0, 2, 2)
        c_turn(0, 0, 2)
        exps(3)
        relu2(1)
        sub2(2)
        sub1(3)
        c_copy(0, 2, 2, "s")
        mean2(1)
        recip(1)
        c_copy(0, 0, 2, "s")
        relu2(2)
        c_quant(0, 0, 4)
        mean2(2)
        product(0, 0, 2)
        gain(1, 0, 4)
        c_turn(1, 2, 2)
        c_turn(1, 0, 2)
        relu1(3)
        recip(2)
        gain(2, 2, 2)
        gain(2, 0, 2)
        c_copy(1, 2, 2, "s")
        sub2(3, 1024, 2048)
        product(0, 2, 2)
        c_copy(1, 0, 2, "s")
        c_turn(2, 2, 2)
        c_quant(1, 0, 4)
        c_copy(2, 2, 2, "s")
        c_turn(2, 0, 2)
        sub2(3, 0, 1024)
        c_copy(2, 0, 2, "s")
        product(1, 0, 2)
        relu2(3, 1024, 2048, "s", 1)
        product(1, 2, 2)
        c_quant(2, 0, 2)
        relu2(3, 0, 1024, "s", 0)
        mean2(3)
        leave(1, 1, "s")
        leave(0, 1, "v")
        c_quant(2, 2, 2)
        leave(0, 0, "s")
        recip(3)
        product(2, 0, 2)
        product(2, 2, 2)
        gain(3, 0, 1)
        gain(3, 1, 1)
        leave(2, 0, "s")
        c_turn(3, 0, 1)
        c_turn(3, 1, 1)
        c_copy(3, 0, 1, "s")
        gain(3, 2, 1)
        c_copy(3, 1, 1, "s")
        c_turn(3, 2, 1)
        leave(1, 0, "s")
        c_copy(3, 2, 1, "s")
        gain(3, 3, 1)
        c_quant(3, 0, 1)
        store(0)
        c_turn(3, 3, 1)
        store(1)
        c_quant(3, 1, 1)
        product(3, 0, 1)
        product(3, 1, 1)
        leave(2, 1, "v")
        c_copy(3, 3, 1, "s")
        c_quant(3, 2, 1)
        product(3, 2, 1)
        store(2)
        c_quant(3, 3, 1)
        product(3, 3, 1)
        leave(3, 0, "s")
        leave(3, 1, "v")
        nc.sync.dma_start(out=out[P * 3 :, 0:512], in_=ot[3][:, 0:512])
        nc.sync.dma_start(out=out[P * 3 :, 512:1024], in_=ot[3][:, 512:1024])
